import numpy as np
import ml_dtypes


def mxq(x, axis, fmt="e4m3"):
    dtype, down = {"e4m3": (ml_dtypes.float8_e4m3fn, 7), "e5m2": (ml_dtypes.float8_e5m2, 14)}[fmt]
    v = np.moveaxis(np.asarray(x, np.float32).astype(ml_dtypes.bfloat16).astype(np.float64), axis, -1)
    blocks = v.reshape(v.shape[:-1] + (-1, 32))
    amax = np.abs(blocks).max(-1, keepdims=True)
    byte = np.maximum(np.where(amax > 0, np.frexp(amax)[1] - 1 + 127, 0) - down, 1)
    scale = np.exp2(byte - 127.0)
    codes = (blocks / scale).astype(np.float32).astype(dtype).astype(np.float64)
    return np.moveaxis((codes * scale).reshape(v.shape), -1, axis)


WIDE = False


def mx_kscale(k):
    if not WIDE:
        return np.ones(k)
    levels = np.array([10, -10, 5, -5, 0])
    if k % 512:
        return np.exp2(np.random.permutation(np.resize(levels, k // 32))).repeat(32)
    a = np.empty((k // 512, 16))
    for p in range(k // 512):
        a[p, :8] = np.random.permutation(np.resize(levels, 8))
        for g in range(8):
            far = levels[np.abs(levels - a[p, g]) >= 10]
            a[p, g + 8] = far[np.random.randint(len(far))]
    return np.exp2(a.ravel()).repeat(32)


def f64(x):
    return np.asarray(x).astype(np.float64)


def striped(idx):
    return np.tile(np.asarray(idx).reshape(-1, 16).T, (8, 1)).astype(np.uint16)


def unstriped(offs):
    return offs[:16].T.reshape(-1).astype(np.int64)


E2M1 = np.array([0.0, 0.5, 1.0, 1.5, 2.0, 3.0, 4.0, 6.0, -0.0, -0.5, -1.0, -1.5, -2.0, -3.0, -4.0, -6.0])


def pack_weight(w, fmt):
    k, n = w.shape
    w = f64(np.asarray(w, np.float32).astype(ml_dtypes.bfloat16)).reshape(k // 32, 32, n)
    amax = np.abs(w).max(1)
    if fmt == "e4m3":
        byte = np.frexp(amax)[1] - 1 + 127 - 7
    else:
        mant, ex = np.frexp(amax / 6.0)
        byte = np.where(mant > 0.5, ex, ex - 1) + 127
    byte = np.clip(np.where(amax > 0, byte, 1), 1, 254)
    scaled = (w * np.exp2(127.0 - byte)[:, None, :]).reshape(k, n).astype(np.float32)
    by_word = np.ascontiguousarray(scaled.reshape(k // 512, 128, 4, n).transpose(0, 1, 3, 2))
    if fmt == "e4m3":
        words = by_word.astype(ml_dtypes.float8_e4m3fn).view(np.uint8)
    else:
        c = by_word.astype(ml_dtypes.float4_e2m1fn).view(np.uint8) & 0xF
        words = (c[..., 0::2] | (c[..., 1::2] << 4)).reshape(k // 512, 128, 2 * n)
    return np.ascontiguousarray(words), np.ascontiguousarray(byte.astype(np.uint8).reshape(k // 512, 16, n))


def unpack_weight(words, scales, fmt):
    g, _, n = scales.shape
    words = np.ascontiguousarray(words).reshape(g, 128, n, -1)
    if fmt == "e4m3":
        vals = words.view(ml_dtypes.float8_e4m3fn).astype(np.float64)
    else:
        nib = np.empty((g, 128, n, 4), np.uint8)
        nib[..., 0::2] = words & 0xF
        nib[..., 1::2] = words >> 4
        vals = E2M1[nib]
    vals = vals * np.repeat(np.exp2(scales.astype(np.float64) - 127.0), 8, axis=1)[..., None]
    return vals.transpose(0, 1, 3, 2).reshape(g * 512, n)


K, T, J, L, S, N = 512, 2048, 512, 512, 1024, 512


def setup_inputs():
    n = np.random.standard_normal
    idx = np.random.permutation(T)[:J]
    idx2 = np.random.permutation(S)[:J]
    fk = mx_kscale(K)
    fl = mx_kscale(L)
    wp = pack_weight(n((K, N)) * 1 / np.sqrt(K) * fk[:, None], "e2m1")
    xbp = pack_weight(n((L, S)) / fl[:, None], "e4m3")
    wbp = pack_weight(n((L, N)) * 1 / np.sqrt(L) * fl[:, None], "e2m1")
    return {
        "xf": (n((K, T))).astype(np.float32),
        "mu": (np.random.uniform(-0.5, 0.5, (K, 1))).astype(np.float32),
        "isd": (np.random.uniform(0.5, 2.0, (K, 1)) / fk[:, None]).astype(np.float32),
        "w_words": wp[0],
        "w_scales": wp[1],
        "xb_words": xbp[0],
        "xb_scales": xbp[1],
        "wb_words": wbp[0],
        "wb_scales": wbp[1],
        "offs": striped(idx),
        "offs2": striped(idx2),
    }


def reference(xf, mu, isd, w_words, w_scales, xb_words, xb_scales, wb_words, wb_scales, offs, offs2):
    idx = unstriped(offs)
    idx2 = unstriped(offs2)
    wu = unpack_weight(w_words, w_scales, "e2m1")
    xbu = unpack_weight(xb_words, xb_scales, "e4m3")
    wbu = unpack_weight(wb_words, wb_scales, "e2m1")
    xs = (f64(xf)[:, idx] - f64(mu)) * f64(isd)
    xsq = mxq(xs, 0, "e4m3")
    p = wu.T @ xsq
    xbidx2g = xbu[:, idx2]
    q = wbu.T @ xbidx2g
    y = np.maximum(p, q)
    return y

@@ -1,0 +1,153 @@
+from contextlib import ExitStack
+
+import concourse.mybir as mybir
+
+K, T, J, L, S, N = 512, 2048, 512, 512, 1024, 512
+FLOPS = 2 * K * N * J + 2 * L * N * J
+
+F32 = mybir.dt.float32
+BF16 = mybir.dt.bfloat16
+I32 = mybir.dt.int32
+U32 = mybir.dt.uint32
+U16 = mybir.dt.uint16
+U8 = mybir.dt.uint8
+FP8X4 = mybir.dt.float8_e4m3fn_x4
+FP4X4 = mybir.dt.float4_e2m1fn_x4
+ALU = mybir.AluOpType
+ACT = mybir.ActivationFunctionType
+
+P = 128
+PACK = 4
+QUADS = 4
+NT = N // P
+HALF = J // 2
+LIST_COL = 16
+
+
+def load_scale_rows(queue, plane, scales):
+    for quad in range(QUADS):
+        queue.dma_start(
+            out=plane[32 * quad : 32 * quad + 4, :].bitcast(I32),
+            in_=scales[0, 4 * quad : 4 * quad + 4, :].bitcast(I32),
+        )
+
+
+def tile_list_standardised_and_raw_kernel(
+    tc, xf, mu, isd, w_words, w_scales, xb_words, xb_scales, wb_words, wb_scales, offs, offs2, out
+):
+    nc = tc.nc
+    with ExitStack() as ctx:
+        keep = ctx.enter_context(tc.tile_pool(name="keep", bufs=1))
+        psum = ctx.enter_context(tc.psum_pool(name="psum", bufs=1))
+
+        list1 = keep.tile([P, J // LIST_COL], U16, name="list1")
+        list2 = keep.tile([P, J // LIST_COL], U16, name="list2")
+        xb_w = keep.tile([P, S], I32, name="xb_w", align_bytes=64)
+        xb_s = keep.tile([P, S], U8, name="xb_s", align_bytes=64)
+        w_w = keep.tile([P, 2 * N], U8, name="w_w", align_bytes=64)
+        wb_w = keep.tile([P, 2 * N], U8, name="wb_w", align_bytes=64)
+        wb_s = keep.tile([P, N], U8, name="wb_s", align_bytes=64)
+        mu_t = keep.tile([P, PACK], F32, name="mu_t")
+        isd_t = keep.tile([P, PACK], F32, name="isd_t")
+        planes = [keep.tile([P, T], F32, name="plane%d" % t, align_bytes=64) for t in range(PACK)]
+        xf_planes = xf.rearrange("(p t) n -> t p n", t=PACK)
+
+        nc.vector.memset(xb_s[:].bitcast(I32), 0)
+        nc.vector.memset(wb_s[:].bitcast(I32), 0)
+
+        nc.gpsimd.dma_start(out=mu_t[:], in_=mu.rearrange("(p t) o -> p (t o)", t=PACK))
+        nc.gpsimd.dma_start(out=isd_t[:], in_=isd.rearrange("(p t) o -> p (t o)", t=PACK))
+        nc.sync.dma_start(list2[:], offs2)
+        nc.sync.dma_start(list1[:], offs)
+        nc.sync.dma_start(out=xb_w[:], in_=xb_words[0].rearrange("p n t -> p (n t)").bitcast(I32))
+        load_scale_rows(nc.sync, xb_s, xb_scales)
+        nc.sync.dma_start(out=planes[0][:], in_=xf_planes[0])
+        load_scale_rows(nc.sync, wb_s, wb_scales)
+        nc.sync.dma_start(out=wb_w[:].bitcast(I32), in_=wb_words[0].bitcast(I32))
+        for t in range(1, PACK):
+            nc.sync.dma_start(out=planes[t][:], in_=xf_planes[t])
+        nc.sync.dma_start(out=w_w[:].bitcast(I32), in_=w_words[0].bitcast(I32))
+
+        neg_mu = keep.tile([P, PACK], F32, name="neg_mu")
+        bias = keep.tile([P, PACK], F32, name="bias")
+        nc.scalar.activation(out=neg_mu[:], in_=mu_t[:], func=ACT.Copy, scale=-1.0)
+        for t in (2, 3):
+            nc.scalar.activation(out=bias[:, t : t + 1], in_=neg_mu[:, t : t + 1], func=ACT.Copy, scale=isd_t[:, t : t + 1])
+
+        xbg_s = keep.tile([P, J], U8, name="xbg_s", align_bytes=64)
+        xbg_w = keep.tile([P, J], U32, name="xbg_w", align_bytes=64)
+        nc.vector.tensor_copy(xbg_w[:], xb_w[:].bitcast(U32).indirect(list2[:]))
+        nc.vector.tensor_copy(xbg_s[:], xb_s[:].indirect(list2[:]))
+        q_sb = keep.tile([P, NT, J], F32, name="q_sb")
+        for nt in range(NT):
+            q_ps = psum.tile([P, J], F32, name="q_ps%d" % nt)
+            nc.tensor.matmul_mx(
+                out=q_ps[:],
+                lhsT=wb_w[:, 2 * P * nt : 2 * P * (nt + 1)].bitcast(FP4X4),
+                lhsT_scale=wb_s[:, P * nt : P * (nt + 1)],
+                rhs=xbg_w[:].bitcast(FP8X4),
+                rhs_scale=xbg_s[:],
+                start=True,
+                stop=True,
+            )
+            nc.scalar.copy(out=q_sb[:, nt, :], in_=q_ps[:])
+
+        w_s = wb_s
+        load_scale_rows(nc.scalar, w_s, w_scales)
+
+        xs = keep.tile([P, J, PACK], BF16, name="xs", align_bytes=64)
+
+        def standardise(t, c0, c1, picked):
+            if t < 2:
+                nc.vector.tensor_scalar(
+                    out=xs[:, c0:c1, t], in0=picked, scalar1=mu_t[:, t : t + 1], scalar2=isd_t[:, t : t + 1],
+                    op0=ALU.subtract, op1=ALU.mult,
+                )
+            else:
+                nc.scalar.activation(
+                    out=xs[:, c0:c1, t], in_=picked, func=ACT.Identity, scale=isd_t[:, t : t + 1], bias=bias[:, t : t + 1]
+                )
+
+        for t in range(PACK - 1):
+            picked = keep.tile([P, J], F32, name="picked%d" % t)
+            nc.vector.tensor_copy(picked[:], planes[t][:].indirect(list1[:]))
+            standardise(t, 0, J, picked[:])
+        cols = HALF // LIST_COL
+        for h in range(2):
+            picked = keep.tile([P, HALF], F32, name="last%d" % h)
+            nc.vector.tensor_copy(picked[:], planes[PACK - 1][:].indirect(list1[:, h * cols : (h + 1) * cols]))
+            for c0 in (0, P):
+                standardise(PACK - 1, h * HALF + c0, h * HALF + c0 + P, picked[:, c0 : c0 + P])
+
+        out_v = out.rearrange("(t p) j -> p t j", p=P)
+        codes = []
+        for h in range(2):
+            xq_w = keep.tile([P, HALF], U32, name="xq_w%d" % h, align_bytes=64)
+            xq_s = keep.tile([P, HALF], U8, name="xq_s%d" % h, align_bytes=64)
+            for c0 in (0, P):
+                nc.vector.quantize_mx(
+                    out=xq_w[:, c0 : c0 + P].bitcast(FP8X4),
+                    scales=xq_s[:, c0 : c0 + P],
+                    in_=xs[:, h * HALF + c0 : h * HALF + c0 + P, :].rearrange("p j t -> p (j t)"),
+                )
+            codes.append((xq_w, xq_s))
+        for h in range(2):
+            xq_w, xq_s = codes[h]
+            for pair in range(NT // 2):
+                p_ps = psum.tile([P, 2, HALF], F32, name="p_ps%d%d" % (h, pair))
+                for i in range(2):
+                    nt = 2 * pair + i
+                    nc.tensor.matmul_mx(
+                        out=p_ps[:, i, :],
+                        lhsT=w_w[:, 2 * P * nt : 2 * P * (nt + 1)].bitcast(FP4X4),
+                        lhsT_scale=w_s[:, P * nt : P * (nt + 1)],
+                        rhs=xq_w[:].bitcast(FP8X4),
+                        rhs_scale=xq_s[:],
+                        start=True,
+                        stop=True,
+                    )
+                res = keep.tile([P, 2, HALF], F32, name="res%d%d" % (h, pair))
+                nc.vector.tensor_tensor(
+                    out=res[:], in0=p_ps[:], in1=q_sb[:, 2 * pair : 2 * pair + 2, h * HALF : (h + 1) * HALF], op=ALU.max
+                )
+                nc.sync.dma_start(out=out_v[:, 2 * pair : 2 * pair + 2, h * HALF : (h + 1) * HALF], in_=res[:])

@@ -57,9 +57,9 @@ def tile_list_standardised_and_raw_kernel(
 
         nc.gpsimd.dma_start(out=mu_t[:], in_=mu.rearrange("(p t) o -> p (t o)", t=PACK))
         nc.gpsimd.dma_start(out=isd_t[:], in_=isd.rearrange("(p t) o -> p (t o)", t=PACK))
+        nc.sync.dma_start(out=xb_w[:], in_=xb_words[0].rearrange("p n t -> p (n t)").bitcast(I32))
         nc.sync.dma_start(list2[:], offs2)
         nc.sync.dma_start(list1[:], offs)
-        nc.sync.dma_start(out=xb_w[:], in_=xb_words[0].rearrange("p n t -> p (n t)").bitcast(I32))
         load_scale_rows(nc.sync, xb_s, xb_scales)
         nc.sync.dma_start(out=planes[0][:], in_=xf_planes[0])
         load_scale_rows(nc.sync, wb_s, wb_scales)
@@ -80,7 +80,7 @@ def tile_list_standardised_and_raw_kernel(
         nc.vector.tensor_copy(xbg_s[:], xb_s[:].indirect(list2[:]))
         q_sb = keep.tile([P, NT, J], F32, name="q_sb")
         for nt in range(NT):
-            q_ps = psum.tile([P, J], F32, name="q_ps%d" % nt)
+            q_ps = psum.tile([P, J], F32, name="q_ps%d" % nt, tag="bank%d" % nt)
             nc.tensor.matmul_mx(
                 out=q_ps[:],
                 lhsT=wb_w[:, 2 * P * nt : 2 * P * (nt + 1)].bitcast(FP4X4),
@@ -93,12 +93,12 @@ def tile_list_standardised_and_raw_kernel(
             nc.scalar.copy(out=q_sb[:, nt, :], in_=q_ps[:])
 
         w_s = wb_s
-        load_scale_rows(nc.scalar, w_s, w_scales)
+        load_scale_rows(nc.sync, w_s, w_scales)
 
         xs = keep.tile([P, J, PACK], BF16, name="xs", align_bytes=64)
 
         def standardise(t, c0, c1, picked):
-            if t < 2:
+            if t < 2 or c0 == P:
                 nc.vector.tensor_scalar(
                     out=xs[:, c0:c1, t], in0=picked, scalar1=mu_t[:, t : t + 1], scalar2=isd_t[:, t : t + 1],
                     op0=ALU.subtract, op1=ALU.mult,
@@ -108,46 +108,51 @@ def tile_list_standardised_and_raw_kernel(
                     out=xs[:, c0:c1, t], in_=picked, func=ACT.Identity, scale=isd_t[:, t : t + 1], bias=bias[:, t : t + 1]
                 )
 
-        for t in range(PACK - 1):
+        for t in range(2):
             picked = keep.tile([P, J], F32, name="picked%d" % t)
             nc.vector.tensor_copy(picked[:], planes[t][:].indirect(list1[:]))
             standardise(t, 0, J, picked[:])
         cols = HALF // LIST_COL
-        for h in range(2):
-            picked = keep.tile([P, HALF], F32, name="last%d" % h)
-            nc.vector.tensor_copy(picked[:], planes[PACK - 1][:].indirect(list1[:, h * cols : (h + 1) * cols]))
-            for c0 in (0, P):
-                standardise(PACK - 1, h * HALF + c0, h * HALF + c0 + P, picked[:, c0 : c0 + P])
+        for t, cuts in ((2, (0, P, HALF, J)), (3, (0, P, HALF, HALF + P, J))):
+            halves = []
+            for h in range(2):
+                picked = keep.tile([P, HALF], F32, name="picked%d%d" % (t, h))
+                nc.vector.tensor_copy(picked[:], planes[t][:].indirect(list1[:, h * cols : (h + 1) * cols]))
+                halves.append(picked)
+            for c0, c1 in zip(cuts, cuts[1:]):
+                h = c0 // HALF
+                standardise(t, c0, c1, halves[h][:, c0 - h * HALF : c1 - h * HALF])
 
         out_v = out.rearrange("(t p) j -> p t j", p=P)
+
+        spans = [(0, P), (P, HALF), (HALF, J)]
         codes = []
-        for h in range(2):
-            xq_w = keep.tile([P, HALF], U32, name="xq_w%d" % h, align_bytes=64)
-            xq_s = keep.tile([P, HALF], U8, name="xq_s%d" % h, align_bytes=64)
-            for c0 in (0, P):
+        for c0, c1 in spans:
+            xq_w = keep.tile([P, c1 - c0], U32, name="xq_w%d" % c0, align_bytes=64)
+            xq_s = keep.tile([P, c1 - c0], U8, name="xq_s%d" % c0, align_bytes=64)
+            for b0 in range(c0, c1, P):
                 nc.vector.quantize_mx(
-                    out=xq_w[:, c0 : c0 + P].bitcast(FP8X4),
-                    scales=xq_s[:, c0 : c0 + P],
-                    in_=xs[:, h * HALF + c0 : h * HALF + c0 + P, :].rearrange("p j t -> p (j t)"),
+                    out=xq_w[:, b0 - c0 : b0 - c0 + P].bitcast(FP8X4),
+                    scales=xq_s[:, b0 - c0 : b0 - c0 + P],
+                    in_=xs[:, b0 : b0 + P, :].rearrange("p j t -> p (j t)"),
                 )
             codes.append((xq_w, xq_s))
-        for h in range(2):
-            xq_w, xq_s = codes[h]
-            for pair in range(NT // 2):
-                p_ps = psum.tile([P, 2, HALF], F32, name="p_ps%d%d" % (h, pair))
-                for i in range(2):
-                    nt = 2 * pair + i
-                    nc.tensor.matmul_mx(
-                        out=p_ps[:, i, :],
-                        lhsT=w_w[:, 2 * P * nt : 2 * P * (nt + 1)].bitcast(FP4X4),
-                        lhsT_scale=w_s[:, P * nt : P * (nt + 1)],
-                        rhs=xq_w[:].bitcast(FP8X4),
-                        rhs_scale=xq_s[:],
-                        start=True,
-                        stop=True,
-                    )
-                res = keep.tile([P, 2, HALF], F32, name="res%d%d" % (h, pair))
-                nc.vector.tensor_tensor(
-                    out=res[:], in0=p_ps[:], in1=q_sb[:, 2 * pair : 2 * pair + 2, h * HALF : (h + 1) * HALF], op=ALU.max
+
+        pieces = [(0, 0, 2), (0, 2, 4), (1, 0, 4), (2, 0, 2), (2, 2, 3), (2, 3, 4)]
+        for i, (span, n0, n1) in enumerate(pieces):
+            c0, c1 = spans[span]
+            xq_w, xq_s = codes[span]
+            p_ps = psum.tile([P, n1 - n0, c1 - c0], F32, name="p_ps%d" % i, tag="bank%d" % ((NT + i) % 8))
+            for nt in range(n0, n1):
+                nc.tensor.matmul_mx(
+                    out=p_ps[:, nt - n0, :],
+                    lhsT=w_w[:, 2 * P * nt : 2 * P * (nt + 1)].bitcast(FP4X4),
+                    lhsT_scale=w_s[:, P * nt : P * (nt + 1)],
+                    rhs=xq_w[:].bitcast(FP8X4),
+                    rhs_scale=xq_s[:],
+                    start=True,
+                    stop=True,
                 )
-                nc.sync.dma_start(out=out_v[:, 2 * pair : 2 * pair + 2, h * HALF : (h + 1) * HALF], in_=res[:])
+            res = keep.tile([P, n1 - n0, c1 - c0], F32, name="res%d" % i)
+            nc.vector.tensor_tensor(out=res[:], in0=p_ps[:], in1=q_sb[:, n0:n1, c0:c1], op=ALU.max)
+            nc.sync.dma_start(out=out_v[:, n0:n1, c0:c1], in_=res[:])

@@ -62,9 +62,10 @@ def tile_list_standardised_and_raw_kernel(
         nc.sync.dma_start(list1[:], offs)
         load_scale_rows(nc.sync, xb_s, xb_scales)
         nc.sync.dma_start(out=planes[0][:], in_=xf_planes[0])
+        nc.sync.dma_start(out=planes[1][:], in_=xf_planes[1])
         load_scale_rows(nc.sync, wb_s, wb_scales)
         nc.sync.dma_start(out=wb_w[:].bitcast(I32), in_=wb_words[0].bitcast(I32))
-        for t in range(1, PACK):
+        for t in range(2, PACK):
             nc.sync.dma_start(out=planes[t][:], in_=xf_planes[t])
         nc.sync.dma_start(out=w_w[:].bitcast(I32), in_=w_words[0].bitcast(I32))
 
@@ -98,7 +99,7 @@ def tile_list_standardised_and_raw_kernel(
         xs = keep.tile([P, J, PACK], BF16, name="xs", align_bytes=64)
 
         def standardise(t, c0, c1, picked):
-            if t < 2 or c0 == P:
+            if t < 2:
                 nc.vector.tensor_scalar(
                     out=xs[:, c0:c1, t], in0=picked, scalar1=mu_t[:, t : t + 1], scalar2=isd_t[:, t : t + 1],
                     op0=ALU.subtract, op1=ALU.mult,
@@ -113,7 +114,7 @@ def tile_list_standardised_and_raw_kernel(
             nc.vector.tensor_copy(picked[:], planes[t][:].indirect(list1[:]))
             standardise(t, 0, J, picked[:])
         cols = HALF // LIST_COL
-        for t, cuts in ((2, (0, P, HALF, J)), (3, (0, P, HALF, HALF + P, J))):
+        for t, cuts in ((2, (0, HALF, J)), (3, (0, P, HALF, HALF + P, J))):
             halves = []
             for h in range(2):
                 picked = keep.tile([P, HALF], F32, name="picked%d%d" % (t, h))
@@ -125,7 +126,7 @@ def tile_list_standardised_and_raw_kernel(
 
         out_v = out.rearrange("(t p) j -> p t j", p=P)
 
-        spans = [(0, P), (P, HALF), (HALF, J)]
+        spans = [(c0, c0 + P) for c0 in range(0, J, P)]
         codes = []
         for c0, c1 in spans:
             xq_w = keep.tile([P, c1 - c0], U32, name="xq_w%d" % c0, align_bytes=64)
@@ -138,7 +139,7 @@ def tile_list_standardised_and_raw_kernel(
                 )
             codes.append((xq_w, xq_s))
 
-        pieces = [(0, 0, 2), (0, 2, 4), (1, 0, 4), (2, 0, 2), (2, 2, 3), (2, 3, 4)]
+        pieces = [(0, 0, 2), (0, 2, 4), (1, 0, 4), (2, 0, 4), (3, 0, 2), (3, 2, 4)]
         for i, (span, n0, n1) in enumerate(pieces):
             c0, c1 = spans[span]
             xq_w, xq_s = codes[span]

from contextlib import ExitStack

import concourse.mybir as mybir

K, T, J, L, S, N = 512, 2048, 512, 512, 1024, 512
FLOPS = 2 * K * N * J + 2 * L * N * J

F32 = mybir.dt.float32
BF16 = mybir.dt.bfloat16
I32 = mybir.dt.int32
U32 = mybir.dt.uint32
U16 = mybir.dt.uint16
U8 = mybir.dt.uint8
FP8X4 = mybir.dt.float8_e4m3fn_x4
FP4X4 = mybir.dt.float4_e2m1fn_x4
ALU = mybir.AluOpType
ACT = mybir.ActivationFunctionType

P = 128
PACK = 4
QUADS = 4
NT = N // P
HALF = J // 2
LIST_COL = 16


def load_scale_rows(queue, plane, scales):
    for quad in range(QUADS):
        queue.dma_start(
            out=plane[32 * quad : 32 * quad + 4, :].bitcast(I32),
            in_=scales[0, 4 * quad : 4 * quad + 4, :].bitcast(I32),
        )


def tile_list_standardised_and_raw_kernel(
    tc, xf, mu, isd, w_words, w_scales, xb_words, xb_scales, wb_words, wb_scales, offs, offs2, out
):
    nc = tc.nc
    with ExitStack() as ctx:
        keep = ctx.enter_context(tc.tile_pool(name="keep", bufs=1))
        psum = ctx.enter_context(tc.psum_pool(name="psum", bufs=1))

        list1 = keep.tile([P, J // LIST_COL], U16, name="list1")
        list2 = keep.tile([P, J // LIST_COL], U16, name="list2")
        xb_w = keep.tile([P, S], I32, name="xb_w", align_bytes=64)
        xb_s = keep.tile([P, S], U8, name="xb_s", align_bytes=64)
        w_w = keep.tile([P, 2 * N], U8, name="w_w", align_bytes=64)
        wb_w = keep.tile([P, 2 * N], U8, name="wb_w", align_bytes=64)
        wb_s = keep.tile([P, N], U8, name="wb_s", align_bytes=64)
        mu_t = keep.tile([P, PACK], F32, name="mu_t")
        isd_t = keep.tile([P, PACK], F32, name="isd_t")
        planes = [keep.tile([P, T], F32, name="plane%d" % t, align_bytes=64) for t in range(PACK)]
        xf_planes = xf.rearrange("(p t) n -> t p n", t=PACK)

        nc.vector.memset(xb_s[:].bitcast(I32), 0)
        nc.vector.memset(wb_s[:].bitcast(I32), 0)

        nc.gpsimd.dma_start(out=mu_t[:], in_=mu.rearrange("(p t) o -> p (t o)", t=PACK))
        nc.gpsimd.dma_start(out=isd_t[:], in_=isd.rearrange("(p t) o -> p (t o)", t=PACK))
        nc.sync.dma_start(out=xb_w[:], in_=xb_words[0].rearrange("p n t -> p (n t)").bitcast(I32))
        nc.sync.dma_start(list2[:], offs2)
        nc.sync.dma_start(list1[:], offs)
        load_scale_rows(nc.sync, xb_s, xb_scales)
        nc.sync.dma_start(out=planes[0][:], in_=xf_planes[0])
        nc.sync.dma_start(out=planes[1][:], in_=xf_planes[1])
        load_scale_rows(nc.sync, wb_s, wb_scales)
        nc.sync.dma_start(out=wb_w[:].bitcast(I32), in_=wb_words[0].bitcast(I32))
        for t in range(2, PACK):
            nc.sync.dma_start(out=planes[t][:], in_=xf_planes[t])
        nc.sync.dma_start(out=w_w[:].bitcast(I32), in_=w_words[0].bitcast(I32))

        neg_mu = keep.tile([P, PACK], F32, name="neg_mu")
        bias = keep.tile([P, PACK], F32, name="bias")
        nc.scalar.activation(out=neg_mu[:], in_=mu_t[:], func=ACT.Copy, scale=-1.0)
        for t in (2, 3):
            nc.scalar.activation(out=bias[:, t : t + 1], in_=neg_mu[:, t : t + 1], func=ACT.Copy, scale=isd_t[:, t : t + 1])

        xbg_s = keep.tile([P, J], U8, name="xbg_s", align_bytes=64)
        xbg_w = keep.tile([P, J], U32, name="xbg_w", align_bytes=64)
        nc.vector.tensor_copy(xbg_w[:], xb_w[:].bitcast(U32).indirect(list2[:]))
        nc.vector.tensor_copy(xbg_s[:], xb_s[:].indirect(list2[:]))
        q_sb = keep.tile([P, NT, J], F32, name="q_sb")
        for nt in range(NT):
            q_ps = psum.tile([P, J], F32, name="q_ps%d" % nt, tag="bank%d" % nt)
            nc.tensor.matmul_mx(
                out=q_ps[:],
                lhsT=wb_w[:, 2 * P * nt : 2 * P * (nt + 1)].bitcast(FP4X4),
                lhsT_scale=wb_s[:, P * nt : P * (nt + 1)],
                rhs=xbg_w[:].bitcast(FP8X4),
                rhs_scale=xbg_s[:],
                start=True,
                stop=True,
            )
            nc.scalar.copy(out=q_sb[:, nt, :], in_=q_ps[:])

        w_s = wb_s
        load_scale_rows(nc.sync, w_s, w_scales)

        xs = keep.tile([P, J, PACK], BF16, name="xs", align_bytes=64)

        def standardise(t, c0, c1, picked):
            if t < 2:
                nc.vector.tensor_scalar(
                    out=xs[:, c0:c1, t], in0=picked, scalar1=mu_t[:, t : t + 1], scalar2=isd_t[:, t : t + 1],
                    op0=ALU.subtract, op1=ALU.mult,
                )
            else:
                nc.scalar.activation(
                    out=xs[:, c0:c1, t], in_=picked, func=ACT.Identity, scale=isd_t[:, t : t + 1], bias=bias[:, t : t + 1]
                )

        for t in range(2):
            picked = keep.tile([P, J], F32, name="picked%d" % t)
            nc.vector.tensor_copy(picked[:], planes[t][:].indirect(list1[:]))
            standardise(t, 0, J, picked[:])
        cols = HALF // LIST_COL
        for t, cuts in ((2, (0, HALF, J)), (3, (0, P, HALF, HALF + P, J))):
            halves = []
            for h in range(2):
                picked = keep.tile([P, HALF], F32, name="picked%d%d" % (t, h))
                nc.vector.tensor_copy(picked[:], planes[t][:].indirect(list1[:, h * cols : (h + 1) * cols]))
                halves.append(picked)
            for c0, c1 in zip(cuts, cuts[1:]):
                h = c0 // HALF
                standardise(t, c0, c1, halves[h][:, c0 - h * HALF : c1 - h * HALF])

        out_v = out.rearrange("(t p) j -> p t j", p=P)

        spans = [(c0, c0 + P) for c0 in range(0, J, P)]
        codes = []
        for c0, c1 in spans:
            xq_w = keep.tile([P, c1 - c0], U32, name="xq_w%d" % c0, align_bytes=64)
            xq_s = keep.tile([P, c1 - c0], U8, name="xq_s%d" % c0, align_bytes=64)
            for b0 in range(c0, c1, P):
                nc.vector.quantize_mx(
                    out=xq_w[:, b0 - c0 : b0 - c0 + P].bitcast(FP8X4),
                    scales=xq_s[:, b0 - c0 : b0 - c0 + P],
                    in_=xs[:, b0 : b0 + P, :].rearrange("p j t -> p (j t)"),
                )
            codes.append((xq_w, xq_s))

        pieces = [(0, 0, 2), (0, 2, 4), (1, 0, 4), (2, 0, 4), (3, 0, 2), (3, 2, 4)]
        for i, (span, n0, n1) in enumerate(pieces):
            c0, c1 = spans[span]
            xq_w, xq_s = codes[span]
            p_ps = psum.tile([P, n1 - n0, c1 - c0], F32, name="p_ps%d" % i, tag="bank%d" % ((NT + i) % 8))
            for nt in range(n0, n1):
                nc.tensor.matmul_mx(
                    out=p_ps[:, nt - n0, :],
                    lhsT=w_w[:, 2 * P * nt : 2 * P * (nt + 1)].bitcast(FP4X4),
                    lhsT_scale=w_s[:, P * nt : P * (nt + 1)],
                    rhs=xq_w[:].bitcast(FP8X4),
                    rhs_scale=xq_s[:],
                    start=True,
                    stop=True,
                )
            res = keep.tile([P, n1 - n0, c1 - c0], F32, name="res%d" % i)
            nc.vector.tensor_tensor(out=res[:], in0=p_ps[:], in1=q_sb[:, n0:n1, c0:c1], op=ALU.max)
            nc.sync.dma_start(out=out_v[:, n0:n1, c0:c1], in_=res[:])
